import numpy as np
import ml_dtypes


def mxq(x, axis, fmt="e4m3"):
    dtype, down = {"e4m3": (ml_dtypes.float8_e4m3fn, 7), "e5m2": (ml_dtypes.float8_e5m2, 14)}[fmt]
    v = np.moveaxis(np.asarray(x, np.float32).astype(ml_dtypes.bfloat16).astype(np.float64), axis, -1)
    blocks = v.reshape(v.shape[:-1] + (-1, 32))
    amax = np.abs(blocks).max(-1, keepdims=True)
    byte = np.maximum(np.where(amax > 0, np.frexp(amax)[1] - 1 + 127, 0) - down, 1)
    scale = np.exp2(byte - 127.0)
    codes = (blocks / scale).astype(np.float32).astype(dtype).astype(np.float64)
    return np.moveaxis((codes * scale).reshape(v.shape), -1, axis)


WIDE = False


def mx_kscale(k):
    if not WIDE:
        return np.ones(k)
    levels = np.array([10, -10, 5, -5, 0])
    if k % 512:
        return np.exp2(np.random.permutation(np.resize(levels, k // 32))).repeat(32)
    a = np.empty((k // 512, 16))
    for p in range(k // 512):
        a[p, :8] = np.random.permutation(np.resize(levels, 8))
        for g in range(8):
            far = levels[np.abs(levels - a[p, g]) >= 10]
            a[p, g + 8] = far[np.random.randint(len(far))]
    return np.exp2(a.ravel()).repeat(32)


def f64(x):
    return np.asarray(x).astype(np.float64)


def striped(idx):
    return np.tile(idx.reshape(-1, 16).T, (8, 1)).astype(np.uint16)


def unstriped(offs):
    return offs[:16].T.reshape(-1).astype(np.int64)


E2M1 = np.array([0.0, 0.5, 1.0, 1.5, 2.0, 3.0, 4.0, 6.0, -0.0, -0.5, -1.0, -1.5, -2.0, -3.0, -4.0, -6.0])


def pack_weight(w, fmt):
    k, n = w.shape
    w = f64(np.asarray(w, np.float32).astype(ml_dtypes.bfloat16)).reshape(k // 32, 32, n)
    amax = np.abs(w).max(1)
    if fmt == "e4m3":
        byte = np.frexp(amax)[1] - 1 + 127 - 7
    else:
        mant, ex = np.frexp(amax / 6.0)
        byte = np.where(mant > 0.5, ex, ex - 1) + 127
    byte = np.clip(np.where(amax > 0, byte, 1), 1, 254)
    scaled = (w * np.exp2(127.0 - byte)[:, None, :]).reshape(k, n).astype(np.float32)
    by_word = np.ascontiguousarray(scaled.reshape(k // 512, 128, 4, n).transpose(0, 1, 3, 2))
    if fmt == "e4m3":
        words = by_word.astype(ml_dtypes.float8_e4m3fn).view(np.uint8)
    else:
        c = by_word.astype(ml_dtypes.float4_e2m1fn).view(np.uint8) & 0xF
        words = (c[..., 0::2] | (c[..., 1::2] << 4)).reshape(k // 512, 128, 2 * n)
    return np.ascontiguousarray(words), np.ascontiguousarray(byte.astype(np.uint8).reshape(k // 512, 16, n))


def unpack_weight(words, scales, fmt):
    g, _, n = scales.shape
    words = np.ascontiguousarray(words).reshape(g, 128, n, -1)
    if fmt == "e4m3":
        vals = words.view(ml_dtypes.float8_e4m3fn).astype(np.float64)
    else:
        nib = np.empty((g, 128, n, 4), np.uint8)
        nib[..., 0::2] = words & 0xF
        nib[..., 1::2] = words >> 4
        vals = E2M1[nib]
    vals = vals * np.repeat(np.exp2(scales.astype(np.float64) - 127.0), 8, axis=1)[..., None]
    return vals.transpose(0, 1, 3, 2).reshape(g * 512, n)


def split(x):
    m, e = np.frexp(f64(x))
    hi = np.ldexp(np.trunc(16.0 * m) / 16.0, e)
    return hi, f64(x) - hi


K, M, T, S = 512, 1024, 4096, 2048


def setup_inputs():
    n = np.random.standard_normal
    s = mx_kscale(K)[:, None]
    v = pack_weight(n((K, T)) * s, "e4m3")
    return {
        "tab_words": v[0],
        "tab_scales": v[1],
        "w": (n((K, M)) / np.sqrt(K) / s).astype(np.float32),
        "rT": n((M, T)).astype(np.float32),
        "b": (0.3 * n(1024)).astype(np.float32),
        "offs": striped(np.random.permutation(T)[:S]),
    }


def reference(tab_words, tab_scales, w, rT, b, offs):
    tab_ = unpack_weight(tab_words, tab_scales, "e4m3")[:, unstriped(offs)]
    w_hi, w_lo = split(w)
    w_hi_, w_lo_ = mxq(w_hi, 0, "e4m3"), mxq(w_lo, 0, "e4m3")
    y = w_hi_.T @ tab_ + w_lo_.T @ tab_
    return (y + f64(b)[:, None]) + f64(rT)[:, unstriped(offs)]

@@ -1,0 +1,130 @@
+from contextlib import ExitStack
+
+import concourse.mybir as mybir
+from concourse.masks import make_identity
+
+K, M, T, S = 512, 1024, 4096, 2048
+FLOPS = 2 * 2 * K * M * S
+
+F32 = mybir.dt.float32
+BF16 = mybir.dt.bfloat16
+I32 = mybir.dt.int32
+U32 = mybir.dt.uint32
+U16 = mybir.dt.uint16
+U8 = mybir.dt.uint8
+FP8X4 = mybir.dt.float8_e4m3fn_x4
+ALU = mybir.AluOpType
+ACT = mybir.ActivationFunctionType
+
+P = 128
+PACK = 4
+BANK = 512
+BLOCKS = M // P
+W_COLS = 512
+HI_MASK_PAIR = 0xFFF0FFF0 - (1 << 32)
+
+
+def tile_list_tabres_bias_kernel(tc, tab_words, tab_scales, w, rT, b, offs, out):
+    nc = tc.nc
+    with ExitStack() as ctx:
+        keep = ctx.enter_context(tc.tile_pool(name="keep", bufs=1))
+        rows = ctx.enter_context(tc.tile_pool(name="rows", bufs=5))
+        res = ctx.enter_context(tc.tile_pool(name="res", bufs=8))
+        prod = ctx.enter_context(tc.tile_pool(name="prod", bufs=2))
+        psum = ctx.enter_context(tc.psum_pool(name="psum", bufs=7))
+        psum_b = ctx.enter_context(tc.psum_pool(name="psum_b", bufs=1))
+
+        offsets = keep.tile([P, S // 16], U16, name="offsets")
+        nc.sync.dma_start(offsets[:], offs)
+
+        tab_s = keep.tile([P, T // 4], I32, name="tab_s", align_bytes=64)
+        nc.vector.memset(tab_s[:], 0)
+        scale_rows = tab_scales[0].bitcast(I32)
+        for r in range(4):
+            nc.sync.dma_start(tab_s[r:P:32, :], scale_rows[r:16:4, :])
+
+        tab_w = keep.tile([P, T], I32, name="tab_w", align_bytes=64)
+        nc.sync.dma_start(tab_w[:], tab_words[0].rearrange("p t i -> p (t i)").bitcast(I32))
+
+        w_rows = w.rearrange("(p t) n -> p t n", t=PACK)
+        w_raw = []
+        for h in range(M // W_COLS):
+            wt = keep.tile([P, PACK, W_COLS], F32, name="w_raw%d" % h, align_bytes=64)
+            nc.sync.dma_start(wt[:], w_rows[:, :, h * W_COLS:(h + 1) * W_COLS])
+            w_raw.append(wt)
+
+        b_rows = keep.tile([P, P], F32, name="b_rows")
+        nc.gpsimd.memset(b_rows[:], 0.0)
+        nc.sync.dma_start(b_rows[0:BLOCKS, :], b.rearrange("(c p) -> c p", p=P))
+        ident = keep.tile([P, P], F32, name="ident")
+        make_identity(nc, ident[:])
+        b_ps = psum_b.tile([P, P], F32, name="b_ps")
+        nc.tensor.transpose(b_ps[:], b_rows[:], ident[:])
+        bias = keep.tile([P, BLOCKS], F32, name="bias")
+        nc.scalar.copy(bias[:], b_ps[:, 0:BLOCKS])
+
+        r_tiles = []
+        for c in range(BLOCKS):
+            rt = rows.tile([P, T], F32, name="rt")
+            nc.sync.dma_start(rt[:], rT[c * P:(c + 1) * P, :])
+            r_tiles.append(rt)
+
+        v_scales = keep.tile([P, S], U8, name="v_scales", align_bytes=64)
+        nc.vector.tensor_copy(v_scales[:], tab_s[:].bitcast(U8).indirect(offsets[:]))
+        v_codes = keep.tile([P, S], U32, name="v_codes", align_bytes=64)
+        nc.vector.tensor_copy(v_codes[:], tab_w[:].bitcast(U32).indirect(offsets[:]))
+
+        hi = res.tile([P, M * PACK], BF16, name="hi", tag="res", align_bytes=64)
+        lo = res.tile([P, M * PACK], BF16, name="lo", tag="res", align_bytes=64)
+        hi_codes = keep.tile([P, M], U32, name="hi_codes", align_bytes=64)
+        lo_codes = keep.tile([P, M], U32, name="lo_codes", align_bytes=64)
+        hi_scales = keep.tile([P, M], U8, name="hi_scales", align_bytes=64)
+        lo_scales = keep.tile([P, M], U8, name="lo_scales", align_bytes=64)
+        for h in range(M // W_COLS):
+            part = slice(h * W_COLS * PACK, (h + 1) * W_COLS * PACK)
+            cols = slice(h * W_COLS, (h + 1) * W_COLS)
+            hi_quads = hi[:, part].rearrange("p (c i t) -> p c t i", i=4, t=PACK)
+            lo_quads = lo[:, part].rearrange("p (c i t) -> p c t i", i=4, t=PACK)
+            upper = w_raw[h][:].bitcast(BF16).rearrange("p t (c i u) -> p c t i u", i=4, u=2)[:, :, :, :, 1]
+            nc.scalar.copy(hi_quads, upper)
+            nc.vector.tensor_scalar(hi[:, part].bitcast(I32), hi[:, part].bitcast(I32), HI_MASK_PAIR, None, ALU.bitwise_and)
+            nc.vector.tensor_tensor(lo_quads, w_raw[h][:].rearrange("p t (c i) -> p c t i", i=4), hi_quads, ALU.subtract)
+            nc.vector.quantize_mx(hi_codes[:, cols].bitcast(FP8X4), hi_scales[:, cols], hi[:, part])
+            nc.vector.quantize_mx(lo_codes[:, cols].bitcast(FP8X4), lo_scales[:, cols], lo[:, part])
+
+        def product(c, s):
+            n_cols = slice(c * P, (c + 1) * P)
+            j_cols = slice(s * BANK, (s + 1) * BANK)
+            acc = psum.tile([P, BANK], F32, name="acc")
+            for first, codes, scales in ((True, hi_codes, hi_scales), (False, lo_codes, lo_scales)):
+                nc.tensor.matmul_mx(
+                    acc[:], lhsT=codes[:, n_cols].bitcast(FP8X4), lhsT_scale=scales[:, n_cols],
+                    rhs=v_codes[:, j_cols].bitcast(FP8X4), rhs_scale=v_scales[:, j_cols],
+                    start=first, stop=not first)
+            return acc
+
+        for c in range(BLOCKS - 1):
+            g = res.tile([P, S], F32, name="g", tag="res", align_bytes=64)
+            nc.vector.tensor_copy(g[:], r_tiles[c][:].indirect(offsets[:]))
+            y = prod.tile([P, S], F32, name="y")
+            for s in range(S // BANK):
+                acc = product(c, s)
+                nc.scalar.activation(y[:, s * BANK:(s + 1) * BANK], acc[:], ACT.Identity, bias=bias[:, c:c + 1], scale=1.0)
+            nc.gpsimd.tensor_tensor(g[:], g[:], y[:], ALU.add)
+            nc.sync.dma_start(out[c * P:(c + 1) * P, :], g[:])
+
+        c = BLOCKS - 1
+        g = res.tile([P, S], F32, name="g_last", tag="res", align_bytes=64)
+
+        def gather_last(s):
+            nc.vector.tensor_copy(g[:, s * BANK:(s + 1) * BANK],
+                                  r_tiles[c][:].indirect(offsets[:, s * BANK // 16:(s + 1) * BANK // 16]))
+
+        gather_last(0)
+        for s in range(S // BANK):
+            j_cols = slice(s * BANK, (s + 1) * BANK)
+            if s + 1 < S // BANK:
+                gather_last(s + 1)
+            acc = product(c, s)
+            nc.vector.scalar_tensor_tensor(g[:, j_cols], acc[:], bias[:, c:c + 1], g[:, j_cols], ALU.add, ALU.add)
+            nc.sync.dma_start(out[c * P:(c + 1) * P, j_cols], g[:, j_cols])

@@ -21,7 +21,7 @@ PACK = 4
 BANK = 512
 BLOCKS = M // P
 W_COLS = 512
-HI_MASK_PAIR = 0xFFF0FFF0 - (1 << 32)
+HI_MASK = 0xFFF00000 - (1 << 32)
 
 
 def tile_list_tabres_bias_kernel(tc, tab_words, tab_scales, w, rT, b, offs, out):
@@ -29,7 +29,7 @@ def tile_list_tabres_bias_kernel(tc, tab_words, tab_scales, w, rT, b, offs, out)
     with ExitStack() as ctx:
         keep = ctx.enter_context(tc.tile_pool(name="keep", bufs=1))
         rows = ctx.enter_context(tc.tile_pool(name="rows", bufs=5))
-        res = ctx.enter_context(tc.tile_pool(name="res", bufs=8))
+        res = ctx.enter_context(tc.tile_pool(name="res", bufs=1))
         prod = ctx.enter_context(tc.tile_pool(name="prod", bufs=2))
         psum = ctx.enter_context(tc.psum_pool(name="psum", bufs=7))
         psum_b = ctx.enter_context(tc.psum_pool(name="psum_b", bufs=1))
@@ -37,21 +37,19 @@ def tile_list_tabres_bias_kernel(tc, tab_words, tab_scales, w, rT, b, offs, out)
         offsets = keep.tile([P, S // 16], U16, name="offsets")
         nc.sync.dma_start(offsets[:], offs)
 
+        w_rows = w.rearrange("(p t) n -> p t n", t=PACK)
+        w_raw = [keep.tile([P, PACK, W_COLS], F32, name="w_raw%d" % h, align_bytes=64) for h in range(M // W_COLS)]
+        nc.sync.dma_start(w_raw[0][:], w_rows[:, :, 0:W_COLS])
+
         tab_s = keep.tile([P, T // 4], I32, name="tab_s", align_bytes=64)
         nc.vector.memset(tab_s[:], 0)
         scale_rows = tab_scales[0].bitcast(I32)
         for r in range(4):
             nc.sync.dma_start(tab_s[r:P:32, :], scale_rows[r:16:4, :])
 
-        tab_w = keep.tile([P, T], I32, name="tab_w", align_bytes=64)
+        nc.sync.dma_start(w_raw[1][:], w_rows[:, :, W_COLS:M])
+        tab_w = keep.tile([P, T], I32, name="tab_w", tag="words", align_bytes=64)
         nc.sync.dma_start(tab_w[:], tab_words[0].rearrange("p t i -> p (t i)").bitcast(I32))
-
-        w_rows = w.rearrange("(p t) n -> p t n", t=PACK)
-        w_raw = []
-        for h in range(M // W_COLS):
-            wt = keep.tile([P, PACK, W_COLS], F32, name="w_raw%d" % h, align_bytes=64)
-            nc.sync.dma_start(wt[:], w_rows[:, :, h * W_COLS:(h + 1) * W_COLS])
-            w_raw.append(wt)
 
         b_rows = keep.tile([P, P], F32, name="b_rows")
         nc.gpsimd.memset(b_rows[:], 0.0)
@@ -69,42 +67,62 @@ def tile_list_tabres_bias_kernel(tc, tab_words, tab_scales, w, rT, b, offs, out)
             nc.sync.dma_start(rt[:], rT[c * P:(c + 1) * P, :])
             r_tiles.append(rt)
 
+        half = W_COLS * PACK
+        w_scales = [keep.tile([P, 2 * W_COLS], U8, name="w_scales%d" % h, align_bytes=64) for h in range(2)]
+
+        def quads_in(ap):
+            return ap.rearrange("p t (c i) -> p c t i", i=4)
+
+        def quads_out(ap):
+            return ap.rearrange("p (c i t) -> p c t i", i=4, t=PACK)
+
+        def high_part(h, hi, split):
+            nc.vector.tensor_scalar(hi[:].bitcast(I32), w_raw[h][:].bitcast(I32), HI_MASK, None, ALU.bitwise_and)
+            nc.scalar.copy(quads_out(split[:, 0:half]), quads_in(hi[:]))
+
+        def low_part(h, hi, split, pieces):
+            width = W_COLS // pieces
+            for n0 in range(0, W_COLS, width):
+                lo = w_raw[h][:, :, n0:n0 + width]
+                nc.gpsimd.tensor_tensor(lo, lo, hi[:, :, n0:n0 + width], ALU.subtract)
+                nc.scalar.copy(quads_out(split[:, half + PACK * n0:half + PACK * (n0 + width)]), quads_in(lo))
+
+        hi0 = res.tile([P, PACK, W_COLS], F32, name="hi0", tag="ring", bufs=6, align_bytes=64)
+        split0 = res.tile([P, 2 * half], BF16, name="split0", tag="slot_a", align_bytes=64)
+        high_part(0, hi0, split0)
+        low_part(0, hi0, split0, 1)
         v_scales = keep.tile([P, S], U8, name="v_scales", align_bytes=64)
         nc.vector.tensor_copy(v_scales[:], tab_s[:].bitcast(U8).indirect(offsets[:]))
+        hi1 = res.tile([P, PACK, W_COLS], F32, name="hi1", tag="ring", bufs=6, align_bytes=64)
+        split1 = res.tile([P, 2 * half], BF16, name="split1", tag="slot_b", align_bytes=64)
+        high_part(1, hi1, split1)
+        low_part(1, hi1, split1, 2)
         v_codes = keep.tile([P, S], U32, name="v_codes", align_bytes=64)
         nc.vector.tensor_copy(v_codes[:], tab_w[:].bitcast(U32).indirect(offsets[:]))
+        both_codes = keep.tile([P, 2, 2 * W_COLS], U32, name="w_codes", tag="words", align_bytes=64)
+        w_codes = [both_codes[:, h, :] for h in range(2)]
+        for h, split in enumerate((split0, split1)):
+            nc.vector.quantize_mx(w_codes[h].bitcast(FP8X4), w_scales[h][:], split[:])
 
-        hi = res.tile([P, M * PACK], BF16, name="hi", tag="res", align_bytes=64)
-        lo = res.tile([P, M * PACK], BF16, name="lo", tag="res", align_bytes=64)
-        hi_codes = keep.tile([P, M], U32, name="hi_codes", align_bytes=64)
-        lo_codes = keep.tile([P, M], U32, name="lo_codes", align_bytes=64)
-        hi_scales = keep.tile([P, M], U8, name="hi_scales", align_bytes=64)
-        lo_scales = keep.tile([P, M], U8, name="lo_scales", align_bytes=64)
-        for h in range(M // W_COLS):
-            part = slice(h * W_COLS * PACK, (h + 1) * W_COLS * PACK)
-            cols = slice(h * W_COLS, (h + 1) * W_COLS)
-            hi_quads = hi[:, part].rearrange("p (c i t) -> p c t i", i=4, t=PACK)
-            lo_quads = lo[:, part].rearrange("p (c i t) -> p c t i", i=4, t=PACK)
-            upper = w_raw[h][:].bitcast(BF16).rearrange("p t (c i u) -> p c t i u", i=4, u=2)[:, :, :, :, 1]
-            nc.scalar.copy(hi_quads, upper)
-            nc.vector.tensor_scalar(hi[:, part].bitcast(I32), hi[:, part].bitcast(I32), HI_MASK_PAIR, None, ALU.bitwise_and)
-            nc.vector.tensor_tensor(lo_quads, w_raw[h][:].rearrange("p t (c i) -> p c t i", i=4), hi_quads, ALU.subtract)
-            nc.vector.quantize_mx(hi_codes[:, cols].bitcast(FP8X4), hi_scales[:, cols], hi[:, part])
-            nc.vector.quantize_mx(lo_codes[:, cols].bitcast(FP8X4), lo_scales[:, cols], lo[:, part])
+        def result_tile(c):
+            if c < 2:
+                return res.tile([P, S], F32, name="g%d" % c, tag=("slot_b", "slot_a")[c], align_bytes=64)
+            return res.tile([P, S], F32, name="g%d" % c, tag="ring", bufs=6, align_bytes=64)
 
         def product(c, s):
-            n_cols = slice(c * P, (c + 1) * P)
+            h, n0 = divmod(c * P, W_COLS)
             j_cols = slice(s * BANK, (s + 1) * BANK)
             acc = psum.tile([P, BANK], F32, name="acc")
-            for first, codes, scales in ((True, hi_codes, hi_scales), (False, lo_codes, lo_scales)):
+            for first in (True, False):
+                n_cols = slice(n0, n0 + P) if first else slice(W_COLS + n0, W_COLS + n0 + P)
                 nc.tensor.matmul_mx(
-                    acc[:], lhsT=codes[:, n_cols].bitcast(FP8X4), lhsT_scale=scales[:, n_cols],
+                    acc[:], lhsT=w_codes[h][:, n_cols].bitcast(FP8X4), lhsT_scale=w_scales[h][:, n_cols],
                     rhs=v_codes[:, j_cols].bitcast(FP8X4), rhs_scale=v_scales[:, j_cols],
                     start=first, stop=not first)
             return acc
 
         for c in range(BLOCKS - 1):
-            g = res.tile([P, S], F32, name="g", tag="res", align_bytes=64)
+            g = result_tile(c)
             nc.vector.tensor_copy(g[:], r_tiles[c][:].indirect(offsets[:]))
             y = prod.tile([P, S], F32, name="y")
             for s in range(S // BANK):
@@ -114,7 +132,7 @@ def tile_list_tabres_bias_kernel(tc, tab_words, tab_scales, w, rT, b, offs, out)
             nc.sync.dma_start(out[c * P:(c + 1) * P, :], g[:])
 
         c = BLOCKS - 1
-        g = res.tile([P, S], F32, name="g_last", tag="res", align_bytes=64)
+        g = result_tile(c)
 
         def gather_last(s):
             nc.vector.tensor_copy(g[:, s * BANK:(s + 1) * BANK],

@@ -34,12 +34,10 @@ def tile_list_tabres_bias_kernel(tc, tab_words, tab_scales, w, rT, b, offs, out)
         psum = ctx.enter_context(tc.psum_pool(name="psum", bufs=7))
         psum_b = ctx.enter_context(tc.psum_pool(name="psum_b", bufs=1))
 
-        offsets = keep.tile([P, S // 16], U16, name="offsets")
-        nc.sync.dma_start(offsets[:], offs)
-
         w_rows = w.rearrange("(p t) n -> p t n", t=PACK)
         w_raw = [keep.tile([P, PACK, W_COLS], F32, name="w_raw%d" % h, align_bytes=64) for h in range(M // W_COLS)]
-        nc.sync.dma_start(w_raw[0][:], w_rows[:, :, 0:W_COLS])
+        for t0 in (0, 2):
+            nc.sync.dma_start(w_raw[0][:, t0:t0 + 2, :], w_rows[:, t0:t0 + 2, 0:W_COLS])
 
         tab_s = keep.tile([P, T // 4], I32, name="tab_s", align_bytes=64)
         nc.vector.memset(tab_s[:], 0)
@@ -47,6 +45,8 @@ def tile_list_tabres_bias_kernel(tc, tab_words, tab_scales, w, rT, b, offs, out)
         for r in range(4):
             nc.sync.dma_start(tab_s[r:P:32, :], scale_rows[r:16:4, :])
 
+        offsets = keep.tile([P, S // 16], U16, name="offsets")
+        nc.sync.dma_start(offsets[:], offs)
         nc.sync.dma_start(w_raw[1][:], w_rows[:, :, W_COLS:M])
         tab_w = keep.tile([P, T], I32, name="tab_w", tag="words", align_bytes=64)
         nc.sync.dma_start(tab_w[:], tab_words[0].rearrange("p t i -> p (t i)").bitcast(I32))
@@ -76,8 +76,10 @@ def tile_list_tabres_bias_kernel(tc, tab_words, tab_scales, w, rT, b, offs, out)
         def quads_out(ap):
             return ap.rearrange("p (c i t) -> p c t i", i=4, t=PACK)
 
-        def high_part(h, hi, split):
-            nc.vector.tensor_scalar(hi[:].bitcast(I32), w_raw[h][:].bitcast(I32), HI_MASK, None, ALU.bitwise_and)
+        def high_part(h, hi, split, planes):
+            for t0 in range(0, PACK, planes):
+                nc.vector.tensor_scalar(hi[:, t0:t0 + planes, :].bitcast(I32), w_raw[h][:, t0:t0 + planes, :].bitcast(I32),
+                                        HI_MASK, None, ALU.bitwise_and)
             nc.scalar.copy(quads_out(split[:, 0:half]), quads_in(hi[:]))
 
         def low_part(h, hi, split, pieces):
@@ -89,13 +91,13 @@ def tile_list_tabres_bias_kernel(tc, tab_words, tab_scales, w, rT, b, offs, out)
 
         hi0 = res.tile([P, PACK, W_COLS], F32, name="hi0", tag="ring", bufs=6, align_bytes=64)
         split0 = res.tile([P, 2 * half], BF16, name="split0", tag="slot_a", align_bytes=64)
-        high_part(0, hi0, split0)
+        high_part(0, hi0, split0, 2)
         low_part(0, hi0, split0, 1)
         v_scales = keep.tile([P, S], U8, name="v_scales", align_bytes=64)
         nc.vector.tensor_copy(v_scales[:], tab_s[:].bitcast(U8).indirect(offsets[:]))
         hi1 = res.tile([P, PACK, W_COLS], F32, name="hi1", tag="ring", bufs=6, align_bytes=64)
         split1 = res.tile([P, 2 * half], BF16, name="split1", tag="slot_b", align_bytes=64)
-        high_part(1, hi1, split1)
+        high_part(1, hi1, split1, 4)
         low_part(1, hi1, split1, 2)
         v_codes = keep.tile([P, S], U32, name="v_codes", align_bytes=64)
         nc.vector.tensor_copy(v_codes[:], tab_w[:].bitcast(U32).indirect(offsets[:]))
@@ -128,8 +130,10 @@ def tile_list_tabres_bias_kernel(tc, tab_words, tab_scales, w, rT, b, offs, out)
             for s in range(S // BANK):
                 acc = product(c, s)
                 nc.scalar.activation(y[:, s * BANK:(s + 1) * BANK], acc[:], ACT.Identity, bias=bias[:, c:c + 1], scale=1.0)
-            nc.gpsimd.tensor_tensor(g[:], g[:], y[:], ALU.add)
-            nc.sync.dma_start(out[c * P:(c + 1) * P, :], g[:])
+            width = S // 2 if c == BLOCKS - 2 else S
+            for j0 in range(0, S, width):
+                nc.gpsimd.tensor_tensor(g[:, j0:j0 + width], g[:, j0:j0 + width], y[:, j0:j0 + width], ALU.add)
+                nc.sync.dma_start(out[c * P:(c + 1) * P, j0:j0 + width], g[:, j0:j0 + width])
 
         c = BLOCKS - 1
         g = result_tile(c)

@@ -35,23 +35,23 @@ def tile_list_tabres_bias_kernel(tc, tab_words, tab_scales, w, rT, b, offs, out)
         psum_b = ctx.enter_context(tc.psum_pool(name="psum_b", bufs=1))
 
         w_rows = w.rearrange("(p t) n -> p t n", t=PACK)
-        w_raw = [keep.tile([P, PACK, W_COLS], F32, name="w_raw%d" % h, align_bytes=64) for h in range(M // W_COLS)]
+        w_raw = [keep.tile([P, PACK, W_COLS], F32, name="w_raw%d" % h, align_bytes=256) for h in range(M // W_COLS)]
         for t0 in (0, 2):
             nc.sync.dma_start(w_raw[0][:, t0:t0 + 2, :], w_rows[:, t0:t0 + 2, 0:W_COLS])
 
-        tab_s = keep.tile([P, T // 4], I32, name="tab_s", align_bytes=64)
+        tab_s = keep.tile([P, T // 4], I32, name="tab_s", align_bytes=256)
         nc.vector.memset(tab_s[:], 0)
         scale_rows = tab_scales[0].bitcast(I32)
         for r in range(4):
             nc.sync.dma_start(tab_s[r:P:32, :], scale_rows[r:16:4, :])
 
-        offsets = keep.tile([P, S // 16], U16, name="offsets")
+        offsets = keep.tile([P, S // 16], U16, name="offsets", align_bytes=256)
         nc.sync.dma_start(offsets[:], offs)
         nc.sync.dma_start(w_raw[1][:], w_rows[:, :, W_COLS:M])
-        tab_w = keep.tile([P, T], I32, name="tab_w", tag="words", align_bytes=64)
+        tab_w = keep.tile([P, T], I32, name="tab_w", tag="words", align_bytes=256)
         nc.sync.dma_start(tab_w[:], tab_words[0].rearrange("p t i -> p (t i)").bitcast(I32))
 
-        b_rows = keep.tile([P, P], F32, name="b_rows")
+        b_rows = keep.tile([P, P], F32, name="b_rows", align_bytes=256)
         nc.gpsimd.memset(b_rows[:], 0.0)
         nc.sync.dma_start(b_rows[0:BLOCKS, :], b.rearrange("(c p) -> c p", p=P))
         ident = keep.tile([P, P], F32, name="ident")
@@ -63,12 +63,12 @@ def tile_list_tabres_bias_kernel(tc, tab_words, tab_scales, w, rT, b, offs, out)
 
         r_tiles = []
         for c in range(BLOCKS):
-            rt = rows.tile([P, T], F32, name="rt")
+            rt = rows.tile([P, T], F32, name="rt", align_bytes=256)
             nc.sync.dma_start(rt[:], rT[c * P:(c + 1) * P, :])
             r_tiles.append(rt)
 
         half = W_COLS * PACK
-        w_scales = [keep.tile([P, 2 * W_COLS], U8, name="w_scales%d" % h, align_bytes=64) for h in range(2)]
+        w_scales = [keep.tile([P, 2 * W_COLS], U8, name="w_scales%d" % h, align_bytes=256) for h in range(2)]
 
         def quads_in(ap):
             return ap.rearrange("p t (c i) -> p c t i", i=4)
@@ -89,27 +89,27 @@ def tile_list_tabres_bias_kernel(tc, tab_words, tab_scales, w, rT, b, offs, out)
                 nc.gpsimd.tensor_tensor(lo, lo, hi[:, :, n0:n0 + width], ALU.subtract)
                 nc.scalar.copy(quads_out(split[:, half + PACK * n0:half + PACK * (n0 + width)]), quads_in(lo))
 
-        hi0 = res.tile([P, PACK, W_COLS], F32, name="hi0", tag="ring", bufs=6, align_bytes=64)
-        split0 = res.tile([P, 2 * half], BF16, name="split0", tag="slot_a", align_bytes=64)
+        hi0 = res.tile([P, PACK, W_COLS], F32, name="hi0", tag="ring", bufs=6, align_bytes=256)
+        split0 = res.tile([P, 2 * half], BF16, name="split0", tag="slot_a", align_bytes=256)
         high_part(0, hi0, split0, 2)
         low_part(0, hi0, split0, 1)
-        v_scales = keep.tile([P, S], U8, name="v_scales", align_bytes=64)
+        v_scales = keep.tile([P, S], U8, name="v_scales", align_bytes=256)
         nc.vector.tensor_copy(v_scales[:], tab_s[:].bitcast(U8).indirect(offsets[:]))
-        hi1 = res.tile([P, PACK, W_COLS], F32, name="hi1", tag="ring", bufs=6, align_bytes=64)
-        split1 = res.tile([P, 2 * half], BF16, name="split1", tag="slot_b", align_bytes=64)
+        hi1 = res.tile([P, PACK, W_COLS], F32, name="hi1", tag="ring", bufs=6, align_bytes=256)
+        split1 = res.tile([P, 2 * half], BF16, name="split1", tag="slot_b", align_bytes=256)
         high_part(1, hi1, split1, 4)
         low_part(1, hi1, split1, 2)
-        v_codes = keep.tile([P, S], U32, name="v_codes", align_bytes=64)
+        v_codes = keep.tile([P, S], U32, name="v_codes", align_bytes=256)
         nc.vector.tensor_copy(v_codes[:], tab_w[:].bitcast(U32).indirect(offsets[:]))
-        both_codes = keep.tile([P, 2, 2 * W_COLS], U32, name="w_codes", tag="words", align_bytes=64)
+        both_codes = keep.tile([P, 2, 2 * W_COLS], U32, name="w_codes", tag="words", align_bytes=256)
         w_codes = [both_codes[:, h, :] for h in range(2)]
         for h, split in enumerate((split0, split1)):
             nc.vector.quantize_mx(w_codes[h].bitcast(FP8X4), w_scales[h][:], split[:])
 
         def result_tile(c):
             if c < 2:
-                return res.tile([P, S], F32, name="g%d" % c, tag=("slot_b", "slot_a")[c], align_bytes=64)
-            return res.tile([P, S], F32, name="g%d" % c, tag="ring", bufs=6, align_bytes=64)
+                return res.tile([P, S], F32, name="g%d" % c, tag=("slot_b", "slot_a")[c], align_bytes=256)
+            return res.tile([P, S], F32, name="g%d" % c, tag="ring", bufs=6, align_bytes=256)
 
         def product(c, s):
             h, n0 = divmod(c * P, W_COLS)

@@ -41,9 +41,7 @@ def tile_list_tabres_bias_kernel(tc, tab_words, tab_scales, w, rT, b, offs, out)
 
         tab_s = keep.tile([P, T // 4], I32, name="tab_s", align_bytes=256)
         nc.vector.memset(tab_s[:], 0)
-        scale_rows = tab_scales[0].bitcast(I32)
-        for r in range(4):
-            nc.sync.dma_start(tab_s[r:P:32, :], scale_rows[r:16:4, :])
+        nc.sync.dma_start(tab_s[32:96:4, :], tab_scales[0].bitcast(I32))
 
         offsets = keep.tile([P, S // 16], U16, name="offsets", align_bytes=256)
         nc.sync.dma_start(offsets[:], offs)
@@ -61,11 +59,18 @@ def tile_list_tabres_bias_kernel(tc, tab_words, tab_scales, w, rT, b, offs, out)
         bias = keep.tile([P, BLOCKS], F32, name="bias")
         nc.scalar.copy(bias[:], b_ps[:, 0:BLOCKS])
 
+        v_scale_words = keep.tile([P, S // 4], I32, name="v_scale_words", align_bytes=256)
+        nc.gpsimd.memset(v_scale_words[:], 0)
+        v_scales = v_scale_words[:].bitcast(U8)
+
         r_tiles = []
-        for c in range(BLOCKS):
+
+        def load_rows(c):
             rt = rows.tile([P, T], F32, name="rt", align_bytes=256)
             nc.sync.dma_start(rt[:], rT[c * P:(c + 1) * P, :])
             r_tiles.append(rt)
+
+        load_rows(0)
 
         half = W_COLS * PACK
         w_scales = [keep.tile([P, 2 * W_COLS], U8, name="w_scales%d" % h, align_bytes=256) for h in range(2)]
@@ -93,8 +98,12 @@ def tile_list_tabres_bias_kernel(tc, tab_words, tab_scales, w, rT, b, offs, out)
         split0 = res.tile([P, 2 * half], BF16, name="split0", tag="slot_a", align_bytes=256)
         high_part(0, hi0, split0, 2)
         low_part(0, hi0, split0, 1)
-        v_scales = keep.tile([P, S], U8, name="v_scales", align_bytes=256)
-        nc.vector.tensor_copy(v_scales[:], tab_s[:].bitcast(U8).indirect(offsets[:]))
+        picked = keep.tile([P, S], U8, name="picked", align_bytes=256)
+        nc.vector.tensor_copy(picked[:], tab_s[:].bitcast(U8).indirect(offsets[:]))
+        for r in range(4):
+            nc.sync.dma_start(v_scale_words[r:P:32, :], picked[32 + 4 * r:96:16, :].bitcast(I32))
+        for c in range(1, BLOCKS):
+            load_rows(c)
         hi1 = res.tile([P, PACK, W_COLS], F32, name="hi1", tag="ring", bufs=6, align_bytes=256)
         split1 = res.tile([P, 2 * half], BF16, name="split1", tag="slot_b", align_bytes=256)
         high_part(1, hi1, split1, 4)

@@ -28,7 +28,7 @@ def tile_list_tabres_bias_kernel(tc, tab_words, tab_scales, w, rT, b, offs, out)
     nc = tc.nc
     with ExitStack() as ctx:
         keep = ctx.enter_context(tc.tile_pool(name="keep", bufs=1))
-        rows = ctx.enter_context(tc.tile_pool(name="rows", bufs=5))
+        rows = ctx.enter_context(tc.tile_pool(name="rows", bufs=6))
         res = ctx.enter_context(tc.tile_pool(name="res", bufs=1))
         prod = ctx.enter_context(tc.tile_pool(name="prod", bufs=2))
         psum = ctx.enter_context(tc.psum_pool(name="psum", bufs=7))

@@ -19,9 +19,13 @@ ACT = mybir.ActivationFunctionType
 P = 128
 PACK = 4
 BANK = 512
+BANKS = S // BANK
+ROWS = 4
+HALF = P * ROWS
 BLOCKS = M // P
-W_COLS = 512
 HI_MASK = 0xFFF00000 - (1 << 32)
+BIAS_ROW = 20
+KIB = 1024
 
 
 def tile_list_tabres_bias_kernel(tc, tab_words, tab_scales, w, rT, b, offs, out):
@@ -29,133 +33,149 @@ def tile_list_tabres_bias_kernel(tc, tab_words, tab_scales, w, rT, b, offs, out)
     with ExitStack() as ctx:
         keep = ctx.enter_context(tc.tile_pool(name="keep", bufs=1))
         rows = ctx.enter_context(tc.tile_pool(name="rows", bufs=6))
-        res = ctx.enter_context(tc.tile_pool(name="res", bufs=1))
-        prod = ctx.enter_context(tc.tile_pool(name="prod", bufs=2))
-        psum = ctx.enter_context(tc.psum_pool(name="psum", bufs=7))
-        psum_b = ctx.enter_context(tc.psum_pool(name="psum_b", bufs=1))
+        laid = ctx.enter_context(tc.tile_pool(name="laid", bufs=1))
+        psum = ctx.enter_context(tc.psum_pool(name="psum", bufs=8))
 
-        w_rows = w.rearrange("(p t) n -> p t n", t=PACK)
-        w_raw = [keep.tile([P, PACK, W_COLS], F32, name="w_raw%d" % h, align_bytes=256) for h in range(M // W_COLS)]
-        for t0 in (0, 2):
-            nc.sync.dma_start(w_raw[0][:, t0:t0 + 2, :], w_rows[:, t0:t0 + 2, 0:W_COLS])
+        def lay(name, shape, dtype, kib):
+            return laid.tile(shape, dtype, name=name, offset=kib * KIB, align_bytes=256)
 
-        tab_s = keep.tile([P, T // 4], I32, name="tab_s", align_bytes=256)
-        nc.vector.memset(tab_s[:], 0)
-        nc.sync.dma_start(tab_s[32:96:4, :], tab_scales[0].bitcast(I32))
-
+        w_planes = w.rearrange("(p t) n -> p t n", t=PACK)
+        w_raw = lay("w_raw", [P, PACK, M], F32, 32)
+        hi = lay("hi", [P, 2, PACK, HALF], F32, 48)
+        lo = lay("lo", [P, 2, PACK, HALF], F32, 64)
+        tab_w = lay("tab_w", [P, T], I32, 80)
+        split = [lay("split%d" % h, [P, 2, ROWS, P, PACK], BF16, 96 + 8 * h) for h in range(2)]
+        tab_s = lay("tab_s", [P, T // 4], I32, 112)
+        picked = lay("picked", [P, S], U8, 116)
+        b_row = lay("b_row", [P, M], F32, 118)
         offsets = keep.tile([P, S // 16], U16, name="offsets", align_bytes=256)
-        nc.sync.dma_start(offsets[:], offs)
-        nc.sync.dma_start(w_raw[1][:], w_rows[:, :, W_COLS:M])
-        tab_w = keep.tile([P, T], I32, name="tab_w", tag="words", align_bytes=256)
-        nc.sync.dma_start(tab_w[:], tab_words[0].rearrange("p t i -> p (t i)").bitcast(I32))
-
-        b_rows = keep.tile([P, P], F32, name="b_rows", align_bytes=256)
-        nc.gpsimd.memset(b_rows[:], 0.0)
-        nc.sync.dma_start(b_rows[0:BLOCKS, :], b.rearrange("(c p) -> c p", p=P))
-        ident = keep.tile([P, P], F32, name="ident")
-        make_identity(nc, ident[:])
-        b_ps = psum_b.tile([P, P], F32, name="b_ps")
-        nc.tensor.transpose(b_ps[:], b_rows[:], ident[:])
-        bias = keep.tile([P, BLOCKS], F32, name="bias")
-        nc.scalar.copy(bias[:], b_ps[:, 0:BLOCKS])
-
         v_scale_words = keep.tile([P, S // 4], I32, name="v_scale_words", align_bytes=256)
-        nc.gpsimd.memset(v_scale_words[:], 0)
         v_scales = v_scale_words[:].bitcast(U8)
+        v_codes = keep.tile([P, S], U32, name="v_codes", align_bytes=256)
+        w_scales = [keep.tile([P, 2 * HALF], U8, name="w_scales%d" % h, align_bytes=256) for h in range(2)]
+        ident = keep.tile([P, P], F32, name="ident")
+        bias = keep.tile([P, BLOCKS], F32, name="bias")
 
+        nc.vector.memset(tab_s[:], 0)
+        make_identity(nc, ident[:])
+        nc.gpsimd.memset(b_row[:], 0.0)
+        nc.gpsimd.memset(v_scale_words[:], 0)
+
+        for t in range(2):
+            nc.sync.dma_start(w_raw[:, t, :], w_planes[:, t, :])
+        nc.sync.dma_start(tab_s[32:96:4, :], tab_scales[0].bitcast(I32))
+        nc.sync.dma_start(offsets[:], offs)
+        nc.sync.dma_start(w_raw[:, 2:PACK, :], w_planes[:, 2:PACK, :])
+        nc.sync.dma_start(tab_w[:], tab_words[0].rearrange("p t i -> p (t i)").bitcast(I32))
+        nc.sync.dma_start(b_row[BIAS_ROW:BIAS_ROW + 1, :], b.rearrange("(o n) -> o n", o=1))
+
+        r_rows = rT.rearrange("(h p i) t -> h i p t", h=2, i=ROWS)
+        out_rows = out.rearrange("(h p i) j -> h p (i j)", h=2, i=ROWS)
         r_tiles = []
 
         def load_rows(c):
             rt = rows.tile([P, T], F32, name="rt", align_bytes=256)
-            nc.sync.dma_start(rt[:], rT[c * P:(c + 1) * P, :])
+            nc.sync.dma_start(rt[:], r_rows[c // ROWS, c % ROWS])
             r_tiles.append(rt)
 
         load_rows(0)
 
-        half = W_COLS * PACK
-        w_scales = [keep.tile([P, 2 * W_COLS], U8, name="w_scales%d" % h, align_bytes=256) for h in range(2)]
+        def by_halves(t0, t1):
+            return w_raw[:, t0:t1, :].rearrange("p t (h n) -> p h t n", h=2)
 
-        def quads_in(ap):
-            return ap.rearrange("p t (c i) -> p c t i", i=4)
+        def mask(t0, t1):
+            nc.vector.tensor_scalar(hi[:, :, t0:t1, :].bitcast(I32), by_halves(t0, t1).bitcast(I32),
+                                    HI_MASK, None, ALU.bitwise_and)
 
-        def quads_out(ap):
-            return ap.rearrange("p (c i t) -> p c t i", i=4, t=PACK)
+        def weave(dst, src):
+            nc.scalar.copy(dst.rearrange("p i q t -> p q t i"), src.rearrange("p t (q i) -> p q t i", i=ROWS))
 
-        def high_part(h, hi, split, planes):
-            for t0 in range(0, PACK, planes):
-                nc.vector.tensor_scalar(hi[:, t0:t0 + planes, :].bitcast(I32), w_raw[h][:, t0:t0 + planes, :].bitcast(I32),
-                                        HI_MASK, None, ALU.bitwise_and)
-            nc.scalar.copy(quads_out(split[:, 0:half]), quads_in(hi[:]))
-
-        def low_part(h, hi, split, pieces):
-            width = W_COLS // pieces
-            for n0 in range(0, W_COLS, width):
-                lo = w_raw[h][:, :, n0:n0 + width]
-                nc.gpsimd.tensor_tensor(lo, lo, hi[:, :, n0:n0 + width], ALU.subtract)
-                nc.scalar.copy(quads_out(split[:, half + PACK * n0:half + PACK * (n0 + width)]), quads_in(lo))
-
-        hi0 = res.tile([P, PACK, W_COLS], F32, name="hi0", tag="ring", bufs=6, align_bytes=256)
-        split0 = res.tile([P, 2 * half], BF16, name="split0", tag="slot_a", align_bytes=256)
-        high_part(0, hi0, split0, 2)
-        low_part(0, hi0, split0, 1)
-        picked = keep.tile([P, S], U8, name="picked", align_bytes=256)
+        mask(0, 1)
+        mask(1, 2)
+        nc.gpsimd.tensor_tensor(lo[:, :, 0:2, :], by_halves(0, 2), hi[:, :, 0:2, :], ALU.subtract)
         nc.vector.tensor_copy(picked[:], tab_s[:].bitcast(U8).indirect(offsets[:]))
         for r in range(4):
             nc.sync.dma_start(v_scale_words[r:P:32, :], picked[32 + 4 * r:96:16, :].bitcast(I32))
         for c in range(1, BLOCKS):
             load_rows(c)
-        hi1 = res.tile([P, PACK, W_COLS], F32, name="hi1", tag="ring", bufs=6, align_bytes=256)
-        split1 = res.tile([P, 2 * half], BF16, name="split1", tag="slot_b", align_bytes=256)
-        high_part(1, hi1, split1, 4)
-        low_part(1, hi1, split1, 2)
-        v_codes = keep.tile([P, S], U32, name="v_codes", align_bytes=256)
+        mask(2, PACK)
         nc.vector.tensor_copy(v_codes[:], tab_w[:].bitcast(U32).indirect(offsets[:]))
-        both_codes = keep.tile([P, 2, 2 * W_COLS], U32, name="w_codes", tag="words", align_bytes=256)
-        w_codes = [both_codes[:, h, :] for h in range(2)]
-        for h, split in enumerate((split0, split1)):
-            nc.vector.quantize_mx(w_codes[h].bitcast(FP8X4), w_scales[h][:], split[:])
+        for h in range(2):
+            nc.gpsimd.tensor_tensor(lo[:, h, 2:PACK, :], w_raw[:, 2:PACK, h * HALF:(h + 1) * HALF],
+                                    hi[:, h, 2:PACK, :], ALU.subtract)
+        for h in range(2):
+            weave(split[h][:, 0], hi[:, h])
+            weave(split[h][:, 1], lo[:, h])
+        w_codes = [lay("w_codes%d" % h, [P, 2 * HALF], U32, 80 + 4 * h) for h in range(2)]
+        for h in range(2):
+            nc.vector.quantize_mx(w_codes[h][:].bitcast(FP8X4), w_scales[h][:],
+                                  split[h][:].rearrange("p a i q t -> p (a i q t)"))
 
-        def result_tile(c):
-            if c < 2:
-                return res.tile([P, S], F32, name="g%d" % c, tag=("slot_b", "slot_a")[c], align_bytes=256)
-            return res.tile([P, S], F32, name="g%d" % c, tag="ring", bufs=6, align_bytes=256)
+        for h in range(2):
+            b_ps = psum.tile([P, BANK], F32, name="acc")
+            for i in range(ROWS):
+                nc.tensor.transpose(b_ps[:, i * P:(i + 1) * P], b_row[:, h * HALF + i:(h + 1) * HALF:ROWS], ident[:])
+            nc.scalar.copy(bias[:, h * ROWS:(h + 1) * ROWS], b_ps[:, BIAS_ROW:BANK:P])
+
+        result = [lay("result%d" % h, [P, ROWS * S], F32, 32 * h) for h in range(2)]
 
         def product(c, s):
-            h, n0 = divmod(c * P, W_COLS)
+            h, i = divmod(c, ROWS)
             j_cols = slice(s * BANK, (s + 1) * BANK)
             acc = psum.tile([P, BANK], F32, name="acc")
-            for first in (True, False):
-                n_cols = slice(n0, n0 + P) if first else slice(W_COLS + n0, W_COLS + n0 + P)
+            for part in range(2):
+                n_cols = slice(part * HALF + i * P, part * HALF + (i + 1) * P)
                 nc.tensor.matmul_mx(
                     acc[:], lhsT=w_codes[h][:, n_cols].bitcast(FP8X4), lhsT_scale=w_scales[h][:, n_cols],
                     rhs=v_codes[:, j_cols].bitcast(FP8X4), rhs_scale=v_scales[:, j_cols],
-                    start=first, stop=not first)
+                    start=part == 0, stop=part == 1)
             return acc
 
+        def cols(c, j0, j1):
+            return result[c // ROWS][:, (c % ROWS) * S + j0:(c % ROWS) * S + j1]
+
+        def gather(c, j0, j1):
+            nc.vector.tensor_copy(cols(c, j0, j1), r_tiles[c][:].indirect(offsets[:, j0 // 16:j1 // 16]))
+
+        def biased(y, c, s):
+            nc.scalar.activation(y, product(c, s)[:], ACT.Identity, bias=bias[:, c:c + 1], scale=1.0)
+
+        def store(c, j0, width):
+            start = (c % ROWS) * S + j0
+            nc.sync.dma_start(out_rows[c // ROWS, :, start:start + width], result[c // ROWS][:, start:start + width])
+
+        def add_on_gpsimd(c, j0, j1, y):
+            nc.gpsimd.tensor_tensor(cols(c, j0, j1), cols(c, j0, j1), y, ALU.add)
+
+        def add_on_vector(c, s):
+            part = cols(c, s * BANK, (s + 1) * BANK)
+            nc.vector.scalar_tensor_tensor(part, product(c, s)[:], bias[:, c:c + 1], part, ALU.add, ALU.add)
+
         for c in range(BLOCKS - 1):
-            g = result_tile(c)
-            nc.vector.tensor_copy(g[:], r_tiles[c][:].indirect(offsets[:]))
-            y = prod.tile([P, S], F32, name="y")
-            for s in range(S // BANK):
-                acc = product(c, s)
-                nc.scalar.activation(y[:, s * BANK:(s + 1) * BANK], acc[:], ACT.Identity, bias=bias[:, c:c + 1], scale=1.0)
-            width = S // 2 if c == BLOCKS - 2 else S
-            for j0 in range(0, S, width):
-                nc.gpsimd.tensor_tensor(g[:, j0:j0 + width], g[:, j0:j0 + width], y[:, j0:j0 + width], ALU.add)
-                nc.sync.dma_start(out[c * P:(c + 1) * P, j0:j0 + width], g[:, j0:j0 + width])
+            gather(c, 0, S)
+            y = lay("y%d" % c, [P, S], F32, 96 + 8 * (c % 2))
+            for s in range(BANKS):
+                biased(y[:, s * BANK:(s + 1) * BANK], c, s)
+            if c < BLOCKS - 2:
+                add_on_gpsimd(c, 0, S, y[:])
+                if c == ROWS - 1:
+                    store(0, 0, ROWS * S)
+                if c >= ROWS:
+                    store(c, 0, S)
+            else:
+                add_on_gpsimd(c, 0, S // 2, y[:, 0:S // 2])
+                store(c, 0, S // 2)
+                add_on_gpsimd(c, S // 2, S, y[:, S // 2:S])
 
         c = BLOCKS - 1
-        g = result_tile(c)
-
-        def gather_last(s):
-            nc.vector.tensor_copy(g[:, s * BANK:(s + 1) * BANK],
-                                  r_tiles[c][:].indirect(offsets[:, s * BANK // 16:(s + 1) * BANK // 16]))
-
-        gather_last(0)
-        for s in range(S // BANK):
-            j_cols = slice(s * BANK, (s + 1) * BANK)
-            if s + 1 < S // BANK:
-                gather_last(s + 1)
-            acc = product(c, s)
-            nc.vector.scalar_tensor_tensor(g[:, j_cols], acc[:], bias[:, c:c + 1], g[:, j_cols], ALU.add, ALU.add)
-            nc.sync.dma_start(out[c * P:(c + 1) * P, j_cols], g[:, j_cols])
+        y = lay("y_last", [P, BANK], F32, 64)
+        gather(c, 0, 2 * BANK)
+        gather(c, 2 * BANK, 3 * BANK)
+        biased(y[:], c, 2)
+        add_on_gpsimd(c, 2 * BANK, 3 * BANK, y[:])
+        add_on_vector(c, 0)
+        add_on_vector(c, 1)
+        store(c - 1, S // 2, S)
+        gather(c, 3 * BANK, S)
+        add_on_vector(c, 3)
+        store(c, S // 2, S // 2)

@@ -160,8 +160,8 @@ def tile_list_tabres_bias_kernel(tc, tab_words, tab_scales, w, rT, b, offs, out)
                 add_on_gpsimd(c, 0, S, y[:])
                 if c == ROWS - 1:
                     store(0, 0, ROWS * S)
-                if c >= ROWS:
-                    store(c, 0, S)
+                if c == ROWS + 1:
+                    store(ROWS, 0, 2 * S)
             else:
                 add_on_gpsimd(c, 0, S // 2, y[:, 0:S // 2])
                 store(c, 0, S // 2)

@@ -26,13 +26,14 @@ BLOCKS = M // P
 HI_MASK = 0xFFF00000 - (1 << 32)
 BIAS_ROW = 20
 KIB = 1024
+R_BUFS = 6
+R_AT = 122
 
 
 def tile_list_tabres_bias_kernel(tc, tab_words, tab_scales, w, rT, b, offs, out):
     nc = tc.nc
     with ExitStack() as ctx:
         keep = ctx.enter_context(tc.tile_pool(name="keep", bufs=1))
-        rows = ctx.enter_context(tc.tile_pool(name="rows", bufs=6))
         laid = ctx.enter_context(tc.tile_pool(name="laid", bufs=1))
         psum = ctx.enter_context(tc.psum_pool(name="psum", bufs=8))
 
@@ -45,7 +46,7 @@ def tile_list_tabres_bias_kernel(tc, tab_words, tab_scales, w, rT, b, offs, out)
         lo = lay("lo", [P, 2, PACK, HALF], F32, 64)
         tab_w = lay("tab_w", [P, T], I32, 80)
         split = [lay("split%d" % h, [P, 2, ROWS, P, PACK], BF16, 96 + 8 * h) for h in range(2)]
-        tab_s = lay("tab_s", [P, T // 4], I32, 112)
+        tab_s = lay("tab_s", [P, T // 4], I32, R_AT + 16)
         picked = lay("picked", [P, S], U8, 116)
         b_row = lay("b_row", [P, M], F32, 118)
         offsets = keep.tile([P, S // 16], U16, name="offsets", align_bytes=256)
@@ -74,7 +75,7 @@ def tile_list_tabres_bias_kernel(tc, tab_words, tab_scales, w, rT, b, offs, out)
         r_tiles = []
 
         def load_rows(c):
-            rt = rows.tile([P, T], F32, name="rt", align_bytes=256)
+            rt = lay("rt%d" % c, [P, T], F32, R_AT + 16 * (c % R_BUFS))
             nc.sync.dma_start(rt[:], r_rows[c // ROWS, c % ROWS])
             r_tiles.append(rt)
 
@@ -95,8 +96,8 @@ def tile_list_tabres_bias_kernel(tc, tab_words, tab_scales, w, rT, b, offs, out)
         nc.gpsimd.tensor_tensor(lo[:, :, 0:2, :], by_halves(0, 2), hi[:, :, 0:2, :], ALU.subtract)
         nc.vector.tensor_copy(picked[:], tab_s[:].bitcast(U8).indirect(offsets[:]))
         for r in range(4):
-            nc.sync.dma_start(v_scale_words[r:P:32, :], picked[32 + 4 * r:96:16, :].bitcast(I32))
-        for c in range(1, BLOCKS):
+            nc.scalar.dma_start(v_scale_words[r:P:32, :], picked[32 + 4 * r:96:16, :].bitcast(I32))
+        for c in range(1, R_BUFS):
             load_rows(c)
         mask(2, PACK)
         nc.vector.tensor_copy(v_codes[:], tab_w[:].bitcast(U32).indirect(offsets[:]))
@@ -153,6 +154,8 @@ def tile_list_tabres_bias_kernel(tc, tab_words, tab_scales, w, rT, b, offs, out)
 
         for c in range(BLOCKS - 1):
             gather(c, 0, S)
+            if c + R_BUFS < BLOCKS:
+                load_rows(c + R_BUFS)
             y = lay("y%d" % c, [P, S], F32, 96 + 8 * (c % 2))
             for s in range(BANKS):
                 biased(y[:, s * BANK:(s + 1) * BANK], c, s)

from contextlib import ExitStack

import concourse.mybir as mybir
from concourse.masks import make_identity

K, M, T, S = 512, 1024, 4096, 2048
FLOPS = 2 * 2 * K * M * S

F32 = mybir.dt.float32
BF16 = mybir.dt.bfloat16
I32 = mybir.dt.int32
U32 = mybir.dt.uint32
U16 = mybir.dt.uint16
U8 = mybir.dt.uint8
FP8X4 = mybir.dt.float8_e4m3fn_x4
ALU = mybir.AluOpType
ACT = mybir.ActivationFunctionType

P = 128
PACK = 4
BANK = 512
BANKS = S // BANK
ROWS = 4
HALF = P * ROWS
BLOCKS = M // P
HI_MASK = 0xFFF00000 - (1 << 32)
BIAS_ROW = 20
KIB = 1024
R_BUFS = 6
R_AT = 122


def tile_list_tabres_bias_kernel(tc, tab_words, tab_scales, w, rT, b, offs, out):
    nc = tc.nc
    with ExitStack() as ctx:
        keep = ctx.enter_context(tc.tile_pool(name="keep", bufs=1))
        laid = ctx.enter_context(tc.tile_pool(name="laid", bufs=1))
        psum = ctx.enter_context(tc.psum_pool(name="psum", bufs=8))

        def lay(name, shape, dtype, kib):
            return laid.tile(shape, dtype, name=name, offset=kib * KIB, align_bytes=256)

        w_planes = w.rearrange("(p t) n -> p t n", t=PACK)
        w_raw = lay("w_raw", [P, PACK, M], F32, 32)
        hi = lay("hi", [P, 2, PACK, HALF], F32, 48)
        lo = lay("lo", [P, 2, PACK, HALF], F32, 64)
        tab_w = lay("tab_w", [P, T], I32, 80)
        split = [lay("split%d" % h, [P, 2, ROWS, P, PACK], BF16, 96 + 8 * h) for h in range(2)]
        tab_s = lay("tab_s", [P, T // 4], I32, R_AT + 16)
        picked = lay("picked", [P, S], U8, 116)
        b_row = lay("b_row", [P, M], F32, 118)
        offsets = keep.tile([P, S // 16], U16, name="offsets", align_bytes=256)
        v_scale_words = keep.tile([P, S // 4], I32, name="v_scale_words", align_bytes=256)
        v_scales = v_scale_words[:].bitcast(U8)
        v_codes = keep.tile([P, S], U32, name="v_codes", align_bytes=256)
        w_scales = [keep.tile([P, 2 * HALF], U8, name="w_scales%d" % h, align_bytes=256) for h in range(2)]
        ident = keep.tile([P, P], F32, name="ident")
        bias = keep.tile([P, BLOCKS], F32, name="bias")

        nc.vector.memset(tab_s[:], 0)
        make_identity(nc, ident[:])
        nc.gpsimd.memset(b_row[:], 0.0)
        nc.gpsimd.memset(v_scale_words[:], 0)

        for t in range(2):
            nc.sync.dma_start(w_raw[:, t, :], w_planes[:, t, :])
        nc.sync.dma_start(tab_s[32:96:4, :], tab_scales[0].bitcast(I32))
        nc.sync.dma_start(offsets[:], offs)
        nc.sync.dma_start(w_raw[:, 2:PACK, :], w_planes[:, 2:PACK, :])
        nc.sync.dma_start(tab_w[:], tab_words[0].rearrange("p t i -> p (t i)").bitcast(I32))
        nc.sync.dma_start(b_row[BIAS_ROW:BIAS_ROW + 1, :], b.rearrange("(o n) -> o n", o=1))

        r_rows = rT.rearrange("(h p i) t -> h i p t", h=2, i=ROWS)
        out_rows = out.rearrange("(h p i) j -> h p (i j)", h=2, i=ROWS)
        r_tiles = []

        def load_rows(c):
            rt = lay("rt%d" % c, [P, T], F32, R_AT + 16 * (c % R_BUFS))
            nc.sync.dma_start(rt[:], r_rows[c // ROWS, c % ROWS])
            r_tiles.append(rt)

        load_rows(0)

        def by_halves(t0, t1):
            return w_raw[:, t0:t1, :].rearrange("p t (h n) -> p h t n", h=2)

        def mask(t0, t1):
            nc.vector.tensor_scalar(hi[:, :, t0:t1, :].bitcast(I32), by_halves(t0, t1).bitcast(I32),
                                    HI_MASK, None, ALU.bitwise_and)

        def weave(dst, src):
            nc.scalar.copy(dst.rearrange("p i q t -> p q t i"), src.rearrange("p t (q i) -> p q t i", i=ROWS))

        mask(0, 1)
        mask(1, 2)
        nc.gpsimd.tensor_tensor(lo[:, :, 0:2, :], by_halves(0, 2), hi[:, :, 0:2, :], ALU.subtract)
        nc.vector.tensor_copy(picked[:], tab_s[:].bitcast(U8).indirect(offsets[:]))
        for r in range(4):
            nc.scalar.dma_start(v_scale_words[r:P:32, :], picked[32 + 4 * r:96:16, :].bitcast(I32))
        for c in range(1, R_BUFS):
            load_rows(c)
        mask(2, PACK)
        nc.vector.tensor_copy(v_codes[:], tab_w[:].bitcast(U32).indirect(offsets[:]))
        for h in range(2):
            nc.gpsimd.tensor_tensor(lo[:, h, 2:PACK, :], w_raw[:, 2:PACK, h * HALF:(h + 1) * HALF],
                                    hi[:, h, 2:PACK, :], ALU.subtract)
        for h in range(2):
            weave(split[h][:, 0], hi[:, h])
            weave(split[h][:, 1], lo[:, h])
        w_codes = [lay("w_codes%d" % h, [P, 2 * HALF], U32, 80 + 4 * h) for h in range(2)]
        for h in range(2):
            nc.vector.quantize_mx(w_codes[h][:].bitcast(FP8X4), w_scales[h][:],
                                  split[h][:].rearrange("p a i q t -> p (a i q t)"))

        for h in range(2):
            b_ps = psum.tile([P, BANK], F32, name="acc")
            for i in range(ROWS):
                nc.tensor.transpose(b_ps[:, i * P:(i + 1) * P], b_row[:, h * HALF + i:(h + 1) * HALF:ROWS], ident[:])
            nc.scalar.copy(bias[:, h * ROWS:(h + 1) * ROWS], b_ps[:, BIAS_ROW:BANK:P])

        result = [lay("result%d" % h, [P, ROWS * S], F32, 32 * h) for h in range(2)]

        def product(c, s):
            h, i = divmod(c, ROWS)
            j_cols = slice(s * BANK, (s + 1) * BANK)
            acc = psum.tile([P, BANK], F32, name="acc")
            for part in range(2):
                n_cols = slice(part * HALF + i * P, part * HALF + (i + 1) * P)
                nc.tensor.matmul_mx(
                    acc[:], lhsT=w_codes[h][:, n_cols].bitcast(FP8X4), lhsT_scale=w_scales[h][:, n_cols],
                    rhs=v_codes[:, j_cols].bitcast(FP8X4), rhs_scale=v_scales[:, j_cols],
                    start=part == 0, stop=part == 1)
            return acc

        def cols(c, j0, j1):
            return result[c // ROWS][:, (c % ROWS) * S + j0:(c % ROWS) * S + j1]

        def gather(c, j0, j1):
            nc.vector.tensor_copy(cols(c, j0, j1), r_tiles[c][:].indirect(offsets[:, j0 // 16:j1 // 16]))

        def biased(y, c, s):
            nc.scalar.activation(y, product(c, s)[:], ACT.Identity, bias=bias[:, c:c + 1], scale=1.0)

        def store(c, j0, width):
            start = (c % ROWS) * S + j0
            nc.sync.dma_start(out_rows[c // ROWS, :, start:start + width], result[c // ROWS][:, start:start + width])

        def add_on_gpsimd(c, j0, j1, y):
            nc.gpsimd.tensor_tensor(cols(c, j0, j1), cols(c, j0, j1), y, ALU.add)

        def add_on_vector(c, s):
            part = cols(c, s * BANK, (s + 1) * BANK)
            nc.vector.scalar_tensor_tensor(part, product(c, s)[:], bias[:, c:c + 1], part, ALU.add, ALU.add)

        for c in range(BLOCKS - 1):
            gather(c, 0, S)
            if c + R_BUFS < BLOCKS:
                load_rows(c + R_BUFS)
            y = lay("y%d" % c, [P, S], F32, 96 + 8 * (c % 2))
            for s in range(BANKS):
                biased(y[:, s * BANK:(s + 1) * BANK], c, s)
            if c < BLOCKS - 2:
                add_on_gpsimd(c, 0, S, y[:])
                if c == ROWS - 1:
                    store(0, 0, ROWS * S)
                if c == ROWS + 1:
                    store(ROWS, 0, 2 * S)
            else:
                add_on_gpsimd(c, 0, S // 2, y[:, 0:S // 2])
                store(c, 0, S // 2)
                add_on_gpsimd(c, S // 2, S, y[:, S // 2:S])

        c = BLOCKS - 1
        y = lay("y_last", [P, BANK], F32, 64)
        gather(c, 0, 2 * BANK)
        gather(c, 2 * BANK, 3 * BANK)
        biased(y[:], c, 2)
        add_on_gpsimd(c, 2 * BANK, 3 * BANK, y[:])
        add_on_vector(c, 0)
        add_on_vector(c, 1)
        store(c - 1, S // 2, S)
        gather(c, 3 * BANK, S)
        add_on_vector(c, 3)
        store(c, S // 2, S // 2)
